import numpy as np, ml_dtypes
CORES = [120,124,248,252,376,380,504,508]
N = 8
F = 32
B1, B2, LR, EPS = 0.75, 0.875, 2.0, 0.001
def setup_inputs(rng):
    idle = rng.random((128, N * F)) < 0.125; ib = np.stack([idle[:, F * r:F * r + F] for r in range(N)])
    return {"gr": (rng.standard_normal((N, 128, N * F), dtype=np.float32) * ~idle).astype(ml_dtypes.bfloat16), "m": (rng.standard_normal((N, 128, F), dtype=np.float32) * np.where(ib, 0.004, 1.0)).astype(ml_dtypes.bfloat16), "v": np.where(ib, 2e-6 * 50 ** rng.random((N, 128, F)), (0.5 + rng.standard_normal((N, 128, F), dtype=np.float32) ** 2) * N).astype(ml_dtypes.bfloat16), "w": rng.standard_normal((N, 128, F), dtype=np.float32).astype(ml_dtypes.bfloat16)}
def setup_inputs_big(rng):
    d = setup_inputs(rng)
    for k in ("gr", "m", "v", "w"): d[k] = (d[k].astype(np.float32) * 1024.0).astype(d[k].dtype)
    return d
def setup_inputs_small(rng):
    d = setup_inputs(rng)
    for k in ("gr", "m", "v", "w"): d[k] = (d[k].astype(np.float32) * (1 / 1024.0)).astype(d[k].dtype)
    return d
def setup_inputs_apart(rng):
    d = setup_inputs(rng)
    f = (10.0 ** rng.permutation(np.linspace(-1.5, 1.5, N))).astype(np.float32).reshape(N, 1, 1)
    for k in ("gr", "m", "v", "w"): d[k] = (d[k].astype(np.float32) * f).astype(d[k].dtype)
    return d
def reference(gr, m, v, w):
    GR, M, V, W = gr.astype(np.float64), m.astype(np.float64), v.astype(np.float64), w.astype(np.float64)
    s = GR.sum(axis=0)
    sb = np.stack([s[:, F * r:F * r + F] for r in range(N)])
    m2 = B1 * M + (1 - B1) * sb
    v2 = B2 * V + (1 - B2) * sb ** 2
    w2 = W - LR * m2 / (np.sqrt(v2) + EPS)
    return {"y": np.broadcast_to(np.concatenate(list(w2), axis=1).astype(ml_dtypes.bfloat16), (N, 128, N * F)), "mo": m2.astype(ml_dtypes.bfloat16), "vo": v2.astype(ml_dtypes.bfloat16)}

@@ -1,0 +1,195 @@
+import math
+from concourse.bass import DstId, RemoteDMATransfer
+from concourse.mybir import AluOpType, ActivationFunctionType
+
+F = 32
+PER_WRITE = 4
+
+SCRATCH = {
+    "g8": ("sbuf", [128, 8, F], "bfloat16"),
+    "pr": ("sbuf", [128, 4, 2, F], "bfloat16"),
+    "l1": ("sbuf", [128, 4, 2, F], "bfloat16"),
+    "l2": ("sbuf", [128, 2, F], "bfloat16"),
+    "mv": ("sbuf", [128, 2, 3 * F], "bfloat16"),
+    "ta": ("sbuf", [128, 2, F], "float32"),
+    "tb": ("sbuf", [128, 2, F], "float32"),
+    "tt": ("sbuf", [128, 2, F], "float32"),
+    "m3": ("sbuf", [128, 2, F], "float32"),
+    "v35": ("sbuf", [128, 2, F], "float32"),
+    "m3t": ("sbuf", [128, 2, F], "float32"),
+    "ss": ("sbuf", [128, 2, F], "float32"),
+    "uu": ("sbuf", [128, 2, F], "float32"),
+    "qq": ("sbuf", [128, 2, F], "float32"),
+    "zz": ("sbuf", [128, 2, F], "float32"),
+    "rr": ("sbuf", [128, 2, F], "float32"),
+    "dd": ("sbuf", [128, 2, F], "float32"),
+    "rc": ("sbuf", [128, 2, F], "float32"),
+    "pp": ("sbuf", [128, 2, F], "float32"),
+    "mob": ("sbuf", [128, F], "bfloat16"),
+    "vob": ("sbuf", [128, F], "bfloat16"),
+    "yl": ("sbuf", [128, 4, 2, F], "bfloat16"),
+    "yb": ("sbuf", [128, 8, F], "bfloat16"),
+}
+SEMAPHORES = ["ldg", "ldmv", "pm", "a1", "amv", "a2", "a3", "sent", "t1", "t2", "e1", "e2", "c1", "cu", "c2", "c3", "c4",
+              "c5", "c6", "c7", "cw", "cv", "up", "smv", "sy"]
+
+
+def _bits(mask):
+    return [e for e in range(mask.bit_length()) if (mask >> e) & 1]
+
+
+def _mask(engines):
+    return sum(1 << e for e in engines)
+
+
+def _plan(T, topo):
+    cores = list(T.cores)
+    rack = [topo.rack(topo.host(c)) for c in cores]
+    pairs = []
+    for a, ca in enumerate(cores):
+        if rack[a] != rack[0]:
+            continue
+        far = [b for b, cb in enumerate(cores)
+               if rack[b] != rack[a] and topo.may_write(ca, cb) and topo.may_write(cb, ca) and topo.die(ca) == topo.die(cb)]
+        pairs.append((a, far[0]))
+    return cores, pairs
+
+
+def _runs(pairs):
+    runs = []
+    for k in range(2):
+        j = 0
+        while j < len(pairs):
+            n = 1
+            while j + n < len(pairs) and pairs[j + n][k] == pairs[j][k] + n:
+                n += 1
+            runs.append((k, j, pairs[j][k], n))
+            j += n
+    return runs
+
+
+def rank_program(g, core, T, topo):
+    rank = T.rank_of(core)
+    if rank is None:
+        return
+    V, S, Q, sem = g.vector, g.scalar, g.sync, T.sem
+    add, sub, mult = AluOpType.add, AluOpType.subtract, AluOpType.mult
+    Act = ActivationFunctionType
+
+    cores, pairs = _plan(T, topo)
+    runs = _runs(pairs)
+    k = 0 if rank in [p[0] for p in pairs] else 1
+    j = [p[k] for p in pairs].index(rank)
+    partner = cores[pairs[j][1 - k]]
+    peers = [(i, cores[p[k]]) for i, p in enumerate(pairs) if i != j]
+    others = [i for i, _ in peers]
+
+    away = [d for _, d in peers if (topo.host(d), topo.chip(d)) != (topo.host(core), topo.chip(core))]
+    away_eng = _bits(topo.mask(core, away[0]))
+    eng, n_away = {}, 0
+    for _, d in peers:
+        if d in away:
+            eng[d] = away_eng[n_away * PER_WRITE:(n_away + 1) * PER_WRITE]
+            n_away += 1
+        else:
+            eng[d] = [e for e in _bits(topo.mask(core, d)) if e not in away_eng][:PER_WRITE]
+    cable_eng = _bits(topo.mask(core, partner))
+    n_group, n_cable = PER_WRITE * len(peers), len(cable_eng)
+
+    def dst(d):
+        rid, pid = topo.addr(d, core)
+        return DstId(rid=rid, pnc=pid)
+
+    def shuffle(to_pairs, done):
+        for n, (kk, j0, b0, cnt) in enumerate(runs):
+            if to_pairs:
+                out, in_ = T.pr[:, j0:j0 + cnt, kk, :], T.g8[:, b0:b0 + cnt, :]
+            else:
+                out, in_ = T.yb[:, b0:b0 + cnt, :], T.yl[:, j0:j0 + cnt, kk, :]
+            if n % 2 == 0:
+                V.tensor_copy(out, in_).then_inc(done, 1)
+            else:
+                S.activation(out, in_, Act.Copy).then_inc(done, 1)
+
+    Q.dma_start(T.g8[:, :, :], T.gr[:, :]).then_inc(sem.ldg, 16)
+    Q.dma_start(T.mv[:, k, 0:F], T.m[:, :]).then_inc(sem.ldmv, 16)
+    Q.dma_start(T.mv[:, k, F:2 * F], T.v[:, :]).then_inc(sem.ldmv, 16)
+    Q.dma_start(T.mv[:, k, 2 * F:3 * F], T.w[:, :]).then_inc(sem.ldmv, 16)
+
+    V.wait_ge(sem.ldg, 16)
+    S.wait_ge(sem.ldg, 16)
+    shuffle(True, sem.pm)
+
+    g.wait_ge(sem.pm, len(runs))
+    g.remote_dma_fused(
+        [RemoteDMATransfer(dst_ids=[dst(d)], dma_engine_mask=_mask(eng[d]), remote_sem=sem.a1,
+                           src=T.pr[:, i, :, :], dst=T.l1[:, j, :, :]) for i, d in peers],
+        local_sem=sem.sent)
+
+    g.wait_ge(sem.ldmv, 48)
+    rid, pid = topo.addr(partner, core)
+    g.remote_dma(T.mv[:, k, :], T.mv[:, k, :], sem.amv, sem.sent, pid, rid, _mask(cable_eng))
+
+    g.wait_ge(sem.a1, n_group)
+    g.remote_dma_fused(
+        [RemoteDMATransfer(dst_ids=[dst(partner)], dma_engine_mask=_mask(cable_eng), remote_sem=sem.a2,
+                           srcs=[T.pr[:, j, :, :]] + [T.l1[:, i, :, :] for i in others], dsts=[T.l2[:, :, :]], alu_op=1)],
+        local_sem=sem.sent)
+
+    V.wait_ge(sem.pm, len(runs))
+    V.wait_ge(sem.a1, n_group)
+    V.tensor_tensor(T.ta[:, :, :], T.pr[:, j, :, :], T.l1[:, others[0], :, :], add).then_inc(sem.t1, 1)
+    V.tensor_tensor(T.tb[:, :, :], T.l1[:, others[1], :, :], T.l1[:, others[2], :, :], add).then_inc(sem.t1, 1)
+    V.wait_ge(sem.t1, 2)
+    V.tensor_tensor(T.tt[:, :, :], T.ta[:, :, :], T.tb[:, :, :], add).then_inc(sem.t2, 1)
+    V.wait_ge(sem.ldmv, 48)
+    V.wait_ge(sem.amv, n_cable)
+    V.tensor_scalar(T.m3[:, :, :], T.mv[:, :, 0:F], 3.0, None, mult).then_inc(sem.e1, 1)
+    V.tensor_scalar(T.v35[:, :, :], T.mv[:, :, F:2 * F], 3.5, None, mult).then_inc(sem.e1, 1)
+    V.wait_ge(sem.t2, 1)
+    V.wait_ge(sem.e1, 2)
+    V.tensor_tensor(T.m3t[:, :, :], T.m3[:, :, :], T.tt[:, :, :], add).then_inc(sem.e2, 1)
+
+    V.wait_ge(sem.a2, n_cable)
+    V.tensor_tensor(T.ss[:, :, :], T.tt[:, :, :], T.l2[:, :, :], add).then_inc(sem.c1, 1)
+    V.wait_ge(sem.e2, 1)
+    V.tensor_tensor(T.uu[:, :, :], T.m3t[:, :, :], T.l2[:, :, :], add).then_inc(sem.cu, 1)
+    S.wait_ge(sem.c1, 1)
+    S.activation(T.qq[:, :, :], T.ss[:, :, :], Act.Square, scale=math.sqrt(0.5)).then_inc(sem.c2, 1)
+    V.wait_ge(sem.c2, 1)
+    V.tensor_tensor(T.zz[:, :, :], T.qq[:, :, :], T.v35[:, :, :], add).then_inc(sem.c3, 1)
+    S.wait_ge(sem.c3, 1)
+    S.activation(T.rr[:, :, :], T.zz[:, :, :], Act.Sqrt).then_inc(sem.c4, 1)
+    V.wait_ge(sem.c4, 1)
+    V.tensor_scalar(T.dd[:, :, :], T.rr[:, :, :], 0.002, None, add).then_inc(sem.c5, 1)
+    V.wait_ge(sem.c5, 1)
+    V.reciprocal(T.rc[:, :, :], T.dd[:, :, :]).then_inc(sem.c6, 1)
+    V.wait_ge(sem.c6, 1)
+    V.wait_ge(sem.cu, 1)
+    V.tensor_tensor(T.pp[:, :, :], T.uu[:, :, :], T.rc[:, :, :], mult).then_inc(sem.c7, 1)
+    V.wait_ge(sem.c7, 1)
+    V.tensor_tensor(T.yl[:, j, :, :], T.mv[:, :, 2 * F:3 * F], T.pp[:, :, :], sub).then_inc(sem.cw, 1)
+
+    S.activation(T.vob[:, :], T.zz[:, k, :], Act.Copy, scale=0.25).then_inc(sem.cv, 1)
+    S.wait_ge(sem.cu, 1)
+    S.activation(T.mob[:, :], T.uu[:, k, :], Act.Copy, scale=0.25).then_inc(sem.cv, 1)
+    Q.wait_ge(sem.cv, 2)
+    Q.dma_start(T.vo[:, :], T.vob[:, :]).then_inc(sem.smv, 16)
+    Q.dma_start(T.mo[:, :], T.mob[:, :]).then_inc(sem.smv, 16)
+
+    g.wait_ge(sem.cw, 1)
+    g.remote_dma_fused(
+        [RemoteDMATransfer(dst_ids=[dst(d)], dma_engine_mask=_mask(eng[d]), remote_sem=sem.a3,
+                           src=T.yl[:, j, :, :], dst=T.yl[:, j, :, :]) for _, d in peers],
+        local_sem=sem.sent)
+
+    V.wait_ge(sem.cw, 1)
+    V.wait_ge(sem.a3, n_group)
+    S.wait_ge(sem.cw, 1)
+    S.wait_ge(sem.a3, n_group)
+    shuffle(False, sem.up)
+    Q.wait_ge(sem.up, len(runs))
+    Q.dma_start(T.y[:, :], T.yb[:, :, :]).then_inc(sem.sy, 16)
+    Q.wait_ge(sem.smv, 32)
+    Q.wait_ge(sem.sy, 16)
+    g.wait_ge(sem.sent, 2 * n_group + 2 * n_cable)

@@ -3,20 +3,17 @@ from concourse.bass import DstId, RemoteDMATransfer
 from concourse.mybir import AluOpType, ActivationFunctionType
 
 F = 32
-PER_WRITE = 4
+R = 2 * F
 
 SCRATCH = {
-    "g8": ("sbuf", [128, 8, F], "bfloat16"),
-    "pr": ("sbuf", [128, 4, 2, F], "bfloat16"),
-    "l1": ("sbuf", [128, 4, 2, F], "bfloat16"),
-    "l2": ("sbuf", [128, 2, F], "bfloat16"),
+    "gd": ("dram", [4, 128, R], "bfloat16"),
+    "l1d": ("dram", [4, 128, R], "bfloat16"),
+    "sa": ("sbuf", [128, 2, F], "bfloat16"),
+    "sb": ("sbuf", [128, 2, F], "bfloat16"),
     "mv": ("sbuf", [128, 2, 3 * F], "bfloat16"),
-    "ta": ("sbuf", [128, 2, F], "float32"),
-    "tb": ("sbuf", [128, 2, F], "float32"),
-    "tt": ("sbuf", [128, 2, F], "float32"),
+    "my": ("sbuf", [128, 3 * F], "bfloat16"),
     "m3": ("sbuf", [128, 2, F], "float32"),
     "v35": ("sbuf", [128, 2, F], "float32"),
-    "m3t": ("sbuf", [128, 2, F], "float32"),
     "ss": ("sbuf", [128, 2, F], "float32"),
     "uu": ("sbuf", [128, 2, F], "float32"),
     "qq": ("sbuf", [128, 2, F], "float32"),
@@ -25,13 +22,12 @@ SCRATCH = {
     "dd": ("sbuf", [128, 2, F], "float32"),
     "rc": ("sbuf", [128, 2, F], "float32"),
     "pp": ("sbuf", [128, 2, F], "float32"),
-    "mob": ("sbuf", [128, F], "bfloat16"),
-    "vob": ("sbuf", [128, F], "bfloat16"),
-    "yl": ("sbuf", [128, 4, 2, F], "bfloat16"),
+    "mvo": ("sbuf", [128, 2, 2, F], "bfloat16"),
+    "mvl": ("sbuf", [128, 2, F], "bfloat16"),
     "yb": ("sbuf", [128, 8, F], "bfloat16"),
 }
-SEMAPHORES = ["ldg", "ldmv", "pm", "a1", "amv", "a2", "a3", "sent", "t1", "t2", "e1", "e2", "c1", "cu", "c2", "c3", "c4",
-              "c5", "c6", "c7", "cw", "cv", "up", "smv", "sy"]
+SEMAPHORES = ["lda", "ldb", "ldc", "ldmv", "a1", "amv", "a2", "a3", "amo", "sent", "s3", "e1", "c1", "cu", "c2", "c3", "c4",
+              "c5", "c6", "c7", "cw", "cv", "smv", "sy"]
 
 
 def _bits(mask):
@@ -42,32 +38,6 @@ def _mask(engines):
     return sum(1 << e for e in engines)
 
 
-def _plan(T, topo):
-    cores = list(T.cores)
-    rack = [topo.rack(topo.host(c)) for c in cores]
-    pairs = []
-    for a, ca in enumerate(cores):
-        if rack[a] != rack[0]:
-            continue
-        far = [b for b, cb in enumerate(cores)
-               if rack[b] != rack[a] and topo.may_write(ca, cb) and topo.may_write(cb, ca) and topo.die(ca) == topo.die(cb)]
-        pairs.append((a, far[0]))
-    return cores, pairs
-
-
-def _runs(pairs):
-    runs = []
-    for k in range(2):
-        j = 0
-        while j < len(pairs):
-            n = 1
-            while j + n < len(pairs) and pairs[j + n][k] == pairs[j][k] + n:
-                n += 1
-            runs.append((k, j, pairs[j][k], n))
-            j += n
-    return runs
-
-
 def rank_program(g, core, T, topo):
     rank = T.rank_of(core)
     if rank is None:
@@ -75,121 +45,149 @@ def rank_program(g, core, T, topo):
     V, S, Q, sem = g.vector, g.scalar, g.sync, T.sem
     add, sub, mult = AluOpType.add, AluOpType.subtract, AluOpType.mult
     Act = ActivationFunctionType
+    cores = list(T.cores)
 
-    cores, pairs = _plan(T, topo)
-    runs = _runs(pairs)
-    k = 0 if rank in [p[0] for p in pairs] else 1
-    j = [p[k] for p in pairs].index(rank)
-    partner = cores[pairs[j][1 - k]]
-    peers = [(i, cores[p[k]]) for i, p in enumerate(pairs) if i != j]
-    others = [i for i, _ in peers]
+    def key(c):
+        return (topo.host(c), topo.chip(c))
 
-    away = [d for _, d in peers if (topo.host(d), topo.chip(d)) != (topo.host(core), topo.chip(core))]
-    away_eng = _bits(topo.mask(core, away[0]))
-    eng, n_away = {}, 0
-    for _, d in peers:
-        if d in away:
-            eng[d] = away_eng[n_away * PER_WRITE:(n_away + 1) * PER_WRITE]
-            n_away += 1
-        else:
-            eng[d] = [e for e in _bits(topo.mask(core, d)) if e not in away_eng][:PER_WRITE]
-    cable_eng = _bits(topo.mask(core, partner))
-    n_group, n_cable = PER_WRITE * len(peers), len(cable_eng)
+    chips = []
+    for c in cores:
+        if key(c) not in chips:
+            chips.append(key(c))
+    members = {ch: [r for r, c in enumerate(cores) if key(c) == ch] for ch in chips}
+    cabled = {}
+    for a in chips:
+        for b in chips:
+            ca, cb = cores[members[a][0]], cores[members[b][0]]
+            if topo.rack(a[0]) != topo.rack(b[0]) and topo.may_write(ca, cb) and topo.may_write(cb, ca):
+                cabled[a] = b
 
-    def dst(d):
-        rid, pid = topo.addr(d, core)
+    def is_lead(r):
+        return topo.die(cores[r]) == topo.die(cores[0])
+
+    def updates(r):
+        return key(cores[r]) if is_lead(r) else cabled[key(cores[r])]
+
+    def collects(r):
+        return cabled[key(cores[r])] if is_lead(r) else key(cores[r])
+
+    ch = key(core)
+    lead = is_lead(rank)
+    idx = members[ch].index(rank)
+    mate = [r for r in members[ch] if r != rank][0]
+    far_same = [r for r in members[cabled[ch]] if topo.die(cores[r]) == topo.die(core)][0]
+    far_upd = [r for r in members[cabled[ch]] if not is_lead(r)][0]
+    mine = [r for r in range(len(cores)) if topo.rack(topo.host(cores[r])) == topo.rack(topo.host(core))]
+    j = mine.index(rank)
+    away = [i for i, r in enumerate(mine) if key(cores[r]) != ch]
+    im = mine.index(mate)
+    b0 = members[updates(rank)][0]
+
+    off_eng = _bits(topo.mask(core, cores[mine[away[0]]]))
+    on_eng = [e for e in _bits(topo.mask(core, cores[mate])) if e not in off_eng]
+    per = len(off_eng) // len(away)
+    eng = {i: off_eng[n * per:(n + 1) * per] for n, i in enumerate(away)}
+    n_off, n_on = len(off_eng), len(on_eng)
+
+    def dst(r):
+        rid, pid = topo.addr(cores[r], core)
         return DstId(rid=rid, pnc=pid)
 
-    def shuffle(to_pairs, done):
-        for n, (kk, j0, b0, cnt) in enumerate(runs):
-            if to_pairs:
-                out, in_ = T.pr[:, j0:j0 + cnt, kk, :], T.g8[:, b0:b0 + cnt, :]
-            else:
-                out, in_ = T.yb[:, b0:b0 + cnt, :], T.yl[:, j0:j0 + cnt, kk, :]
-            if n % 2 == 0:
-                V.tensor_copy(out, in_).then_inc(done, 1)
-            else:
-                S.activation(out, in_, Act.Copy).then_inc(done, 1)
+    def piece(i):
+        c0 = members[collects(mine[i])][0] * F
+        return T.gr[:, c0:c0 + R]
 
-    Q.dma_start(T.g8[:, :, :], T.gr[:, :]).then_inc(sem.ldg, 16)
-    Q.dma_start(T.mv[:, k, 0:F], T.m[:, :]).then_inc(sem.ldmv, 16)
-    Q.dma_start(T.mv[:, k, F:2 * F], T.v[:, :]).then_inc(sem.ldmv, 16)
-    Q.dma_start(T.mv[:, k, 2 * F:3 * F], T.w[:, :]).then_inc(sem.ldmv, 16)
+    for i in away:
+        Q.dma_start(T.gd[i], piece(i)).then_inc(sem.lda, 16)
+    Q.dma_start(T.gd[im], piece(im)).then_inc(sem.ldb, 16)
+    own = T.mv[:, idx, :] if lead else T.my[:, :]
+    for n, t in enumerate((T.m, T.v, T.w)):
+        out = T.mv[:, idx, n * F:(n + 1) * F] if lead else T.my[:, n * F:(n + 1) * F]
+        Q.dma_start(out, t[:, :]).then_inc(sem.ldmv, 16)
+    Q.dma_start(T.gd[j], piece(j)).then_inc(sem.ldc, 16)
 
-    V.wait_ge(sem.ldg, 16)
-    S.wait_ge(sem.ldg, 16)
-    shuffle(True, sem.pm)
-
-    g.wait_ge(sem.pm, len(runs))
+    g.wait_ge(sem.lda, 16 * len(away))
     g.remote_dma_fused(
-        [RemoteDMATransfer(dst_ids=[dst(d)], dma_engine_mask=_mask(eng[d]), remote_sem=sem.a1,
-                           src=T.pr[:, i, :, :], dst=T.l1[:, j, :, :]) for i, d in peers],
+        [RemoteDMATransfer(dst_ids=[dst(mine[i])], dma_engine_mask=_mask(eng[i]), remote_sem=sem.a1,
+                           src=T.gd[i], dst=T.l1d[j]) for i in away],
         local_sem=sem.sent)
+    g.wait_ge(sem.ldb, 16)
+    rid, pid = topo.addr(cores[mate], core)
+    g.remote_dma(T.l1d[j], T.gd[im], sem.a1, sem.sent, pid, rid, _mask(on_eng))
 
     g.wait_ge(sem.ldmv, 48)
-    rid, pid = topo.addr(partner, core)
-    g.remote_dma(T.mv[:, k, :], T.mv[:, k, :], sem.amv, sem.sent, pid, rid, _mask(cable_eng))
+    aside = [RemoteDMATransfer(dst_ids=[dst(far_upd)], dma_engine_mask=_mask(off_eng), remote_sem=sem.amv,
+                               src=own, dst=T.mv[:, idx, :])]
+    if not lead:
+        aside.append(RemoteDMATransfer(dst_ids=[dst(mate)], dma_engine_mask=_mask(on_eng), remote_sem=sem.amv,
+                                       src=own, dst=T.mv[:, idx, :]))
+    g.remote_dma_fused(aside, local_sem=sem.sent)
 
-    g.wait_ge(sem.a1, n_group)
+    g.wait_ge(sem.ldc, 16)
+    g.wait_ge(sem.a1, n_off + n_on)
+    srcs = [T.gd[j]] + [T.l1d[i] for i in range(len(mine)) if i != j]
     g.remote_dma_fused(
-        [RemoteDMATransfer(dst_ids=[dst(partner)], dma_engine_mask=_mask(cable_eng), remote_sem=sem.a2,
-                           srcs=[T.pr[:, j, :, :]] + [T.l1[:, i, :, :] for i in others], dsts=[T.l2[:, :, :]], alu_op=1)],
+        [RemoteDMATransfer(dst_ids=[dst(far_same)], dma_engine_mask=_mask(off_eng), remote_sem=sem.a2,
+                           srcs=srcs, dsts=[T.sb[:, :, :]], alu_op=1),
+         RemoteDMATransfer(dst_ids=[dst(mate)], dma_engine_mask=_mask(on_eng), remote_sem=sem.a2,
+                           srcs=srcs, dsts=[T.sa[:, :, :]], alu_op=1)],
         local_sem=sem.sent)
 
-    V.wait_ge(sem.pm, len(runs))
-    V.wait_ge(sem.a1, n_group)
-    V.tensor_tensor(T.ta[:, :, :], T.pr[:, j, :, :], T.l1[:, others[0], :, :], add).then_inc(sem.t1, 1)
-    V.tensor_tensor(T.tb[:, :, :], T.l1[:, others[1], :, :], T.l1[:, others[2], :, :], add).then_inc(sem.t1, 1)
-    V.wait_ge(sem.t1, 2)
-    V.tensor_tensor(T.tt[:, :, :], T.ta[:, :, :], T.tb[:, :, :], add).then_inc(sem.t2, 1)
-    V.wait_ge(sem.ldmv, 48)
-    V.wait_ge(sem.amv, n_cable)
+    if lead:
+        V.wait_ge(sem.ldmv, 48)
+    V.wait_ge(sem.amv, n_on if lead else 2 * n_off)
     V.tensor_scalar(T.m3[:, :, :], T.mv[:, :, 0:F], 3.0, None, mult).then_inc(sem.e1, 1)
     V.tensor_scalar(T.v35[:, :, :], T.mv[:, :, F:2 * F], 3.5, None, mult).then_inc(sem.e1, 1)
-    V.wait_ge(sem.t2, 1)
-    V.wait_ge(sem.e1, 2)
-    V.tensor_tensor(T.m3t[:, :, :], T.m3[:, :, :], T.tt[:, :, :], add).then_inc(sem.e2, 1)
 
-    V.wait_ge(sem.a2, n_cable)
-    V.tensor_tensor(T.ss[:, :, :], T.tt[:, :, :], T.l2[:, :, :], add).then_inc(sem.c1, 1)
-    V.wait_ge(sem.e2, 1)
-    V.tensor_tensor(T.uu[:, :, :], T.m3t[:, :, :], T.l2[:, :, :], add).then_inc(sem.cu, 1)
+    V.wait_ge(sem.a2, n_off + n_on)
+    V.tensor_tensor(T.ss[:, :, :], T.sa[:, :, :], T.sb[:, :, :], add).then_inc(sem.c1, 1)
     S.wait_ge(sem.c1, 1)
     S.activation(T.qq[:, :, :], T.ss[:, :, :], Act.Square, scale=math.sqrt(0.5)).then_inc(sem.c2, 1)
+    V.wait_ge(sem.e1, 2)
     V.wait_ge(sem.c2, 1)
     V.tensor_tensor(T.zz[:, :, :], T.qq[:, :, :], T.v35[:, :, :], add).then_inc(sem.c3, 1)
     S.wait_ge(sem.c3, 1)
-    S.activation(T.rr[:, :, :], T.zz[:, :, :], Act.Sqrt).then_inc(sem.c4, 1)
+    S.activation(T.rr[:, :, :], T.zz[:, :, :], Act.Sqrt, scale=2.0 ** -20).then_inc(sem.c4, 1)
+    V.wait_ge(sem.c1, 1)
+    V.tensor_tensor(T.uu[:, :, :], T.m3[:, :, :], T.ss[:, :, :], add).then_inc(sem.cu, 1)
+    if lead:
+        V.wait_ge(sem.cu, 1)
+        V.tensor_scalar(T.mvo[:, :, 0, :], T.uu[:, :, :], 0.25, None, mult).then_inc(sem.cv, 1)
+        V.wait_ge(sem.c3, 1)
+        V.tensor_scalar(T.mvo[:, :, 1, :], T.zz[:, :, :], 0.25, None, mult).then_inc(sem.cv, 1)
     V.wait_ge(sem.c4, 1)
-    V.tensor_scalar(T.dd[:, :, :], T.rr[:, :, :], 0.002, None, add).then_inc(sem.c5, 1)
+    V.tensor_scalar(T.dd[:, :, :], T.rr[:, :, :], 1024.0, 0.002, mult, add).then_inc(sem.c5, 1)
     V.wait_ge(sem.c5, 1)
     V.reciprocal(T.rc[:, :, :], T.dd[:, :, :]).then_inc(sem.c6, 1)
     V.wait_ge(sem.c6, 1)
     V.wait_ge(sem.cu, 1)
     V.tensor_tensor(T.pp[:, :, :], T.uu[:, :, :], T.rc[:, :, :], mult).then_inc(sem.c7, 1)
     V.wait_ge(sem.c7, 1)
-    V.tensor_tensor(T.yl[:, j, :, :], T.mv[:, :, 2 * F:3 * F], T.pp[:, :, :], sub).then_inc(sem.cw, 1)
+    V.tensor_tensor(T.yb[:, b0:b0 + 2, :], T.mv[:, :, 2 * F:3 * F], T.pp[:, :, :], sub).then_inc(sem.cw, 1)
 
-    S.activation(T.vob[:, :], T.zz[:, k, :], Act.Copy, scale=0.25).then_inc(sem.cv, 1)
-    S.wait_ge(sem.cu, 1)
-    S.activation(T.mob[:, :], T.uu[:, k, :], Act.Copy, scale=0.25).then_inc(sem.cv, 1)
-    Q.wait_ge(sem.cv, 2)
-    Q.dma_start(T.vo[:, :], T.vob[:, :]).then_inc(sem.smv, 16)
-    Q.dma_start(T.mo[:, :], T.mob[:, :]).then_inc(sem.smv, 16)
+    if lead:
+        g.wait_ge(sem.cv, 2)
+        g.remote_dma(T.mvl[:, :, :], T.mvo[:, 1 - idx, :, :], sem.amo, sem.sent, pid, rid, _mask(on_eng))
+        Q.wait_ge(sem.cv, 2)
+        Q.dma_start(T.mo[:, :], T.mvo[:, idx, 0, :]).then_inc(sem.smv, 16)
+        Q.dma_start(T.vo[:, :], T.mvo[:, idx, 1, :]).then_inc(sem.smv, 16)
 
     g.wait_ge(sem.cw, 1)
     g.remote_dma_fused(
-        [RemoteDMATransfer(dst_ids=[dst(d)], dma_engine_mask=_mask(eng[d]), remote_sem=sem.a3,
-                           src=T.yl[:, j, :, :], dst=T.yl[:, j, :, :]) for _, d in peers],
-        local_sem=sem.sent)
+        [RemoteDMATransfer(dst_ids=[dst(mine[i])], dma_engine_mask=_mask(eng[i] if i in eng else on_eng), remote_sem=sem.a3,
+                           src=T.yb[:, b0:b0 + 2, :], dst=T.yb[:, b0:b0 + 2, :]) for i in range(len(mine)) if i != j],
+        local_sem=sem.s3)
 
-    V.wait_ge(sem.cw, 1)
-    V.wait_ge(sem.a3, n_group)
-    S.wait_ge(sem.cw, 1)
-    S.wait_ge(sem.a3, n_group)
-    shuffle(False, sem.up)
-    Q.wait_ge(sem.up, len(runs))
+    if not lead:
+        Q.wait_ge(sem.amo, n_on)
+        Q.wait_ge(sem.s3, n_off + n_on)
+        Q.dma_start(T.mo[:, :], T.mvl[:, 0, :]).then_inc(sem.smv, 16)
+        Q.dma_start(T.vo[:, :], T.mvl[:, 1, :]).then_inc(sem.smv, 16)
+
+    Q.wait_ge(sem.cw, 1)
+    Q.wait_ge(sem.a3, n_off + n_on)
     Q.dma_start(T.y[:, :], T.yb[:, :, :]).then_inc(sem.sy, 16)
     Q.wait_ge(sem.smv, 32)
     Q.wait_ge(sem.sy, 16)
-    g.wait_ge(sem.sent, 2 * n_group + 2 * n_cable)
+    g.wait_ge(sem.sent, 3 * n_off + 3 * n_on)
+    g.wait_ge(sem.s3, n_off + n_on)

@@ -4,6 +4,10 @@ from concourse.mybir import AluOpType, ActivationFunctionType
 
 F = 32
 R = 2 * F
+E = 0.002
+L = 1024.0
+DL = 2e-6
+C1, C2 = 0.43, 1.09
 
 SCRATCH = {
     "gd": ("dram", [4, 128, R], "bfloat16"),
@@ -13,12 +17,18 @@ SCRATCH = {
     "mv": ("sbuf", [128, 2, 3 * F], "bfloat16"),
     "my": ("sbuf", [128, 3 * F], "bfloat16"),
     "m3": ("sbuf", [128, 2, F], "float32"),
-    "v35": ("sbuf", [128, 2, F], "float32"),
+    "vp": ("sbuf", [128, 2, F], "float32"),
+    "aa": ("sbuf", [128, 2, F], "float32"),
+    "b1": ("sbuf", [128, 2, F], "float32"),
+    "b2": ("sbuf", [128, 2, F], "float32"),
+    "p1": ("sbuf", [128, 2, F], "float32"),
+    "xx": ("sbuf", [128, 2, F], "float32"),
+    "sq": ("sbuf", [128, 2, F], "float32"),
+    "nn": ("sbuf", [128, 2, F], "float32"),
     "ss": ("sbuf", [128, 2, F], "float32"),
     "uu": ("sbuf", [128, 2, F], "float32"),
     "qq": ("sbuf", [128, 2, F], "float32"),
     "zz": ("sbuf", [128, 2, F], "float32"),
-    "rr": ("sbuf", [128, 2, F], "float32"),
     "dd": ("sbuf", [128, 2, F], "float32"),
     "rc": ("sbuf", [128, 2, F], "float32"),
     "pp": ("sbuf", [128, 2, F], "float32"),
@@ -27,7 +37,7 @@ SCRATCH = {
     "yb": ("sbuf", [128, 8, F], "bfloat16"),
 }
 SEMAPHORES = ["lda", "ldb", "ldc", "ldmv", "a1", "amv", "a2", "a3", "amo", "sent", "s3", "e1", "c1", "cu", "c2", "c3", "c4",
-              "c5", "c6", "c7", "cw", "cv", "smv", "sy"]
+              "c5", "c6", "c7", "c8", "c9", "c10", "cr", "cz", "cn", "cw", "cv", "smv", "sy"]
 
 
 def _bits(mask):
@@ -133,44 +143,61 @@ def rank_program(g, core, T, topo):
                            srcs=srcs, dsts=[T.sa[:, :, :]], alu_op=1)],
         local_sem=sem.sent)
 
+    kr, br = 3.5 / (L * L), (DL / L) ** 2
     if lead:
+        S.wait_ge(sem.ldmv, 48)
+        S.activation(T.aa[:, idx, :], T.mv[:, idx, F:2 * F], Act.Sqrt, bias=br, scale=kr).then_inc(sem.cr, 1)
+        S.wait_ge(sem.amv, n_on)
+        S.activation(T.aa[:, 1 - idx, :], T.mv[:, 1 - idx, F:2 * F], Act.Sqrt, bias=br, scale=kr).then_inc(sem.cr, 1)
         V.wait_ge(sem.ldmv, 48)
+    else:
+        S.wait_ge(sem.amv, 2 * n_off)
+        S.activation(T.aa[:, :, :], T.mv[:, :, F:2 * F], Act.Sqrt, bias=br, scale=kr).then_inc(sem.cr, 2)
     V.wait_ge(sem.amv, n_on if lead else 2 * n_off)
     V.tensor_scalar(T.m3[:, :, :], T.mv[:, :, 0:F], 3.0, None, mult).then_inc(sem.e1, 1)
-    V.tensor_scalar(T.v35[:, :, :], T.mv[:, :, F:2 * F], 3.5, None, mult).then_inc(sem.e1, 1)
+    V.tensor_scalar(T.vp[:, :, :], T.mv[:, :, F:2 * F], 3.5 / (2 * L), -E * E / (2 * L), mult, add).then_inc(sem.e1, 1)
 
     V.wait_ge(sem.a2, n_off + n_on)
     V.tensor_tensor(T.ss[:, :, :], T.sa[:, :, :], T.sb[:, :, :], add).then_inc(sem.c1, 1)
     S.wait_ge(sem.c1, 1)
-    S.activation(T.qq[:, :, :], T.ss[:, :, :], Act.Square, scale=math.sqrt(0.5)).then_inc(sem.c2, 1)
-    V.wait_ge(sem.e1, 2)
-    V.wait_ge(sem.c2, 1)
-    V.tensor_tensor(T.zz[:, :, :], T.qq[:, :, :], T.v35[:, :, :], add).then_inc(sem.c3, 1)
-    S.wait_ge(sem.c3, 1)
-    S.activation(T.rr[:, :, :], T.zz[:, :, :], Act.Sqrt, scale=2.0 ** -20).then_inc(sem.c4, 1)
+    S.activation(T.b1[:, :, :], T.ss[:, :, :], Act.Abs, scale=C1 * math.sqrt(0.5) / L).then_inc(sem.c2, 1)
+    S.activation(T.b2[:, :, :], T.ss[:, :, :], Act.Abs, scale=C2 * math.sqrt(0.5) / L).then_inc(sem.c3, 1)
+    S.activation(T.qq[:, :, :], T.ss[:, :, :], Act.Square, scale=math.sqrt(0.25 / L)).then_inc(sem.c4, 1)
     V.wait_ge(sem.c1, 1)
+    V.wait_ge(sem.e1, 2)
     V.tensor_tensor(T.uu[:, :, :], T.m3[:, :, :], T.ss[:, :, :], add).then_inc(sem.cu, 1)
-    if lead:
-        V.wait_ge(sem.cu, 1)
-        V.tensor_scalar(T.mvo[:, :, 0, :], T.uu[:, :, :], 0.25, None, mult).then_inc(sem.cv, 1)
-        V.wait_ge(sem.c3, 1)
-        V.tensor_scalar(T.mvo[:, :, 1, :], T.zz[:, :, :], 0.25, None, mult).then_inc(sem.cv, 1)
-    V.wait_ge(sem.c4, 1)
-    V.tensor_scalar(T.dd[:, :, :], T.rr[:, :, :], 1024.0, 0.002, mult, add).then_inc(sem.c5, 1)
+    V.wait_ge(sem.cr, 2)
+    V.wait_ge(sem.c2, 1)
+    V.tensor_tensor(T.p1[:, :, :], T.aa[:, :, :], T.b1[:, :, :], add).then_inc(sem.c5, 1)
     V.wait_ge(sem.c5, 1)
-    V.reciprocal(T.rc[:, :, :], T.dd[:, :, :]).then_inc(sem.c6, 1)
-    V.wait_ge(sem.c6, 1)
+    V.wait_ge(sem.c3, 1)
+    V.tensor_tensor(T.xx[:, :, :], T.p1[:, :, :], T.b2[:, :, :], AluOpType.max).then_inc(sem.c6, 1)
+    S.wait_ge(sem.c6, 1)
+    S.activation(T.sq[:, :, :], T.xx[:, :, :], Act.Square, bias=E / math.sqrt(2 * L),
+                 scale=L / math.sqrt(2 * L)).then_inc(sem.c7, 1)
+    V.wait_ge(sem.c4, 1)
+    V.tensor_tensor(T.zz[:, :, :], T.qq[:, :, :], T.vp[:, :, :], add).then_inc(sem.cz, 1)
     V.wait_ge(sem.cu, 1)
-    V.tensor_tensor(T.pp[:, :, :], T.uu[:, :, :], T.rc[:, :, :], mult).then_inc(sem.c7, 1)
+    V.wait_ge(sem.c6, 1)
+    V.tensor_tensor(T.nn[:, :, :], T.uu[:, :, :], T.xx[:, :, :], mult).then_inc(sem.cn, 1)
     V.wait_ge(sem.c7, 1)
+    V.wait_ge(sem.cz, 1)
+    V.tensor_tensor(T.dd[:, :, :], T.sq[:, :, :], T.zz[:, :, :], add).then_inc(sem.c8, 1)
+    V.wait_ge(sem.c8, 1)
+    V.reciprocal(T.rc[:, :, :], T.dd[:, :, :]).then_inc(sem.c9, 1)
+    V.wait_ge(sem.c9, 1)
+    V.wait_ge(sem.cn, 1)
+    V.tensor_tensor(T.pp[:, :, :], T.nn[:, :, :], T.rc[:, :, :], mult).then_inc(sem.c10, 1)
+    V.wait_ge(sem.c10, 1)
     V.tensor_tensor(T.yb[:, b0:b0 + 2, :], T.mv[:, :, 2 * F:3 * F], T.pp[:, :, :], sub).then_inc(sem.cw, 1)
 
     if lead:
+        S.wait_ge(sem.cu, 1)
+        S.activation(T.mvo[:, :, 0, :], T.uu[:, :, :], Act.Copy, scale=0.25).then_inc(sem.cv, 1)
+        S.wait_ge(sem.cz, 1)
+        S.activation(T.mvo[:, :, 1, :], T.zz[:, :, :], Act.Identity, bias=E * E / 4, scale=L / 2).then_inc(sem.cv, 1)
         g.wait_ge(sem.cv, 2)
         g.remote_dma(T.mvl[:, :, :], T.mvo[:, 1 - idx, :, :], sem.amo, sem.sent, pid, rid, _mask(on_eng))
-        Q.wait_ge(sem.cv, 2)
-        Q.dma_start(T.mo[:, :], T.mvo[:, idx, 0, :]).then_inc(sem.smv, 16)
-        Q.dma_start(T.vo[:, :], T.mvo[:, idx, 1, :]).then_inc(sem.smv, 16)
 
     g.wait_ge(sem.cw, 1)
     g.remote_dma_fused(
@@ -178,7 +205,12 @@ def rank_program(g, core, T, topo):
                            src=T.yb[:, b0:b0 + 2, :], dst=T.yb[:, b0:b0 + 2, :]) for i in range(len(mine)) if i != j],
         local_sem=sem.s3)
 
-    if not lead:
+    if lead:
+        Q.wait_ge(sem.cv, 2)
+        Q.wait_ge(sem.s3, n_off + n_on)
+        Q.dma_start(T.mo[:, :], T.mvo[:, idx, 0, :]).then_inc(sem.smv, 16)
+        Q.dma_start(T.vo[:, :], T.mvo[:, idx, 1, :]).then_inc(sem.smv, 16)
+    else:
         Q.wait_ge(sem.amo, n_on)
         Q.wait_ge(sem.s3, n_off + n_on)
         Q.dma_start(T.mo[:, :], T.mvl[:, 0, :]).then_inc(sem.smv, 16)

import math
from concourse.bass import DstId, RemoteDMATransfer
from concourse.mybir import AluOpType, ActivationFunctionType

F = 32
R = 2 * F
E = 0.002
L = 1024.0
DL = 2e-6
C1, C2 = 0.43, 1.09

SCRATCH = {
    "gd": ("dram", [4, 128, R], "bfloat16"),
    "l1d": ("dram", [4, 128, R], "bfloat16"),
    "sa": ("sbuf", [128, 2, F], "bfloat16"),
    "sb": ("sbuf", [128, 2, F], "bfloat16"),
    "mv": ("sbuf", [128, 2, 3 * F], "bfloat16"),
    "my": ("sbuf", [128, 3 * F], "bfloat16"),
    "m3": ("sbuf", [128, 2, F], "float32"),
    "vp": ("sbuf", [128, 2, F], "float32"),
    "aa": ("sbuf", [128, 2, F], "float32"),
    "b1": ("sbuf", [128, 2, F], "float32"),
    "b2": ("sbuf", [128, 2, F], "float32"),
    "p1": ("sbuf", [128, 2, F], "float32"),
    "xx": ("sbuf", [128, 2, F], "float32"),
    "sq": ("sbuf", [128, 2, F], "float32"),
    "nn": ("sbuf", [128, 2, F], "float32"),
    "ss": ("sbuf", [128, 2, F], "float32"),
    "uu": ("sbuf", [128, 2, F], "float32"),
    "qq": ("sbuf", [128, 2, F], "float32"),
    "zz": ("sbuf", [128, 2, F], "float32"),
    "dd": ("sbuf", [128, 2, F], "float32"),
    "rc": ("sbuf", [128, 2, F], "float32"),
    "pp": ("sbuf", [128, 2, F], "float32"),
    "mvo": ("sbuf", [128, 2, 2, F], "bfloat16"),
    "mvl": ("sbuf", [128, 2, F], "bfloat16"),
    "yb": ("sbuf", [128, 8, F], "bfloat16"),
}
SEMAPHORES = ["lda", "ldb", "ldc", "ldmv", "a1", "amv", "a2", "a3", "amo", "sent", "s3", "e1", "c1", "cu", "c2", "c3", "c4",
              "c5", "c6", "c7", "c8", "c9", "c10", "cr", "cz", "cn", "cw", "cv", "smv", "sy"]


def _bits(mask):
    return [e for e in range(mask.bit_length()) if (mask >> e) & 1]


def _mask(engines):
    return sum(1 << e for e in engines)


def rank_program(g, core, T, topo):
    rank = T.rank_of(core)
    if rank is None:
        return
    V, S, Q, sem = g.vector, g.scalar, g.sync, T.sem
    add, sub, mult = AluOpType.add, AluOpType.subtract, AluOpType.mult
    Act = ActivationFunctionType
    cores = list(T.cores)

    def key(c):
        return (topo.host(c), topo.chip(c))

    chips = []
    for c in cores:
        if key(c) not in chips:
            chips.append(key(c))
    members = {ch: [r for r, c in enumerate(cores) if key(c) == ch] for ch in chips}
    cabled = {}
    for a in chips:
        for b in chips:
            ca, cb = cores[members[a][0]], cores[members[b][0]]
            if topo.rack(a[0]) != topo.rack(b[0]) and topo.may_write(ca, cb) and topo.may_write(cb, ca):
                cabled[a] = b

    def is_lead(r):
        return topo.die(cores[r]) == topo.die(cores[0])

    def updates(r):
        return key(cores[r]) if is_lead(r) else cabled[key(cores[r])]

    def collects(r):
        return cabled[key(cores[r])] if is_lead(r) else key(cores[r])

    ch = key(core)
    lead = is_lead(rank)
    idx = members[ch].index(rank)
    mate = [r for r in members[ch] if r != rank][0]
    far_same = [r for r in members[cabled[ch]] if topo.die(cores[r]) == topo.die(core)][0]
    far_upd = [r for r in members[cabled[ch]] if not is_lead(r)][0]
    mine = [r for r in range(len(cores)) if topo.rack(topo.host(cores[r])) == topo.rack(topo.host(core))]
    j = mine.index(rank)
    away = [i for i, r in enumerate(mine) if key(cores[r]) != ch]
    im = mine.index(mate)
    b0 = members[updates(rank)][0]

    off_eng = _bits(topo.mask(core, cores[mine[away[0]]]))
    on_eng = [e for e in _bits(topo.mask(core, cores[mate])) if e not in off_eng]
    per = len(off_eng) // len(away)
    eng = {i: off_eng[n * per:(n + 1) * per] for n, i in enumerate(away)}
    n_off, n_on = len(off_eng), len(on_eng)

    def dst(r):
        rid, pid = topo.addr(cores[r], core)
        return DstId(rid=rid, pnc=pid)

    def piece(i):
        c0 = members[collects(mine[i])][0] * F
        return T.gr[:, c0:c0 + R]

    for i in away:
        Q.dma_start(T.gd[i], piece(i)).then_inc(sem.lda, 16)
    Q.dma_start(T.gd[im], piece(im)).then_inc(sem.ldb, 16)
    own = T.mv[:, idx, :] if lead else T.my[:, :]
    for n, t in enumerate((T.m, T.v, T.w)):
        out = T.mv[:, idx, n * F:(n + 1) * F] if lead else T.my[:, n * F:(n + 1) * F]
        Q.dma_start(out, t[:, :]).then_inc(sem.ldmv, 16)
    Q.dma_start(T.gd[j], piece(j)).then_inc(sem.ldc, 16)

    g.wait_ge(sem.lda, 16 * len(away))
    g.remote_dma_fused(
        [RemoteDMATransfer(dst_ids=[dst(mine[i])], dma_engine_mask=_mask(eng[i]), remote_sem=sem.a1,
                           src=T.gd[i], dst=T.l1d[j]) for i in away],
        local_sem=sem.sent)
    g.wait_ge(sem.ldb, 16)
    rid, pid = topo.addr(cores[mate], core)
    g.remote_dma(T.l1d[j], T.gd[im], sem.a1, sem.sent, pid, rid, _mask(on_eng))

    g.wait_ge(sem.ldmv, 48)
    aside = [RemoteDMATransfer(dst_ids=[dst(far_upd)], dma_engine_mask=_mask(off_eng), remote_sem=sem.amv,
                               src=own, dst=T.mv[:, idx, :])]
    if not lead:
        aside.append(RemoteDMATransfer(dst_ids=[dst(mate)], dma_engine_mask=_mask(on_eng), remote_sem=sem.amv,
                                       src=own, dst=T.mv[:, idx, :]))
    g.remote_dma_fused(aside, local_sem=sem.sent)

    g.wait_ge(sem.ldc, 16)
    g.wait_ge(sem.a1, n_off + n_on)
    srcs = [T.gd[j]] + [T.l1d[i] for i in range(len(mine)) if i != j]
    g.remote_dma_fused(
        [RemoteDMATransfer(dst_ids=[dst(far_same)], dma_engine_mask=_mask(off_eng), remote_sem=sem.a2,
                           srcs=srcs, dsts=[T.sb[:, :, :]], alu_op=1),
         RemoteDMATransfer(dst_ids=[dst(mate)], dma_engine_mask=_mask(on_eng), remote_sem=sem.a2,
                           srcs=srcs, dsts=[T.sa[:, :, :]], alu_op=1)],
        local_sem=sem.sent)

    kr, br = 3.5 / (L * L), (DL / L) ** 2
    if lead:
        S.wait_ge(sem.ldmv, 48)
        S.activation(T.aa[:, idx, :], T.mv[:, idx, F:2 * F], Act.Sqrt, bias=br, scale=kr).then_inc(sem.cr, 1)
        S.wait_ge(sem.amv, n_on)
        S.activation(T.aa[:, 1 - idx, :], T.mv[:, 1 - idx, F:2 * F], Act.Sqrt, bias=br, scale=kr).then_inc(sem.cr, 1)
        V.wait_ge(sem.ldmv, 48)
    else:
        S.wait_ge(sem.amv, 2 * n_off)
        S.activation(T.aa[:, :, :], T.mv[:, :, F:2 * F], Act.Sqrt, bias=br, scale=kr).then_inc(sem.cr, 2)
    V.wait_ge(sem.amv, n_on if lead else 2 * n_off)
    V.tensor_scalar(T.m3[:, :, :], T.mv[:, :, 0:F], 3.0, None, mult).then_inc(sem.e1, 1)
    V.tensor_scalar(T.vp[:, :, :], T.mv[:, :, F:2 * F], 3.5 / (2 * L), -E * E / (2 * L), mult, add).then_inc(sem.e1, 1)

    V.wait_ge(sem.a2, n_off + n_on)
    V.tensor_tensor(T.ss[:, :, :], T.sa[:, :, :], T.sb[:, :, :], add).then_inc(sem.c1, 1)
    S.wait_ge(sem.c1, 1)
    S.activation(T.b1[:, :, :], T.ss[:, :, :], Act.Abs, scale=C1 * math.sqrt(0.5) / L).then_inc(sem.c2, 1)
    S.activation(T.b2[:, :, :], T.ss[:, :, :], Act.Abs, scale=C2 * math.sqrt(0.5) / L).then_inc(sem.c3, 1)
    S.activation(T.qq[:, :, :], T.ss[:, :, :], Act.Square, scale=math.sqrt(0.25 / L)).then_inc(sem.c4, 1)
    V.wait_ge(sem.c1, 1)
    V.wait_ge(sem.e1, 2)
    V.tensor_tensor(T.uu[:, :, :], T.m3[:, :, :], T.ss[:, :, :], add).then_inc(sem.cu, 1)
    V.wait_ge(sem.cr, 2)
    V.wait_ge(sem.c2, 1)
    V.tensor_tensor(T.p1[:, :, :], T.aa[:, :, :], T.b1[:, :, :], add).then_inc(sem.c5, 1)
    V.wait_ge(sem.c5, 1)
    V.wait_ge(sem.c3, 1)
    V.tensor_tensor(T.xx[:, :, :], T.p1[:, :, :], T.b2[:, :, :], AluOpType.max).then_inc(sem.c6, 1)
    S.wait_ge(sem.c6, 1)
    S.activation(T.sq[:, :, :], T.xx[:, :, :], Act.Square, bias=E / math.sqrt(2 * L),
                 scale=L / math.sqrt(2 * L)).then_inc(sem.c7, 1)
    V.wait_ge(sem.c4, 1)
    V.tensor_tensor(T.zz[:, :, :], T.qq[:, :, :], T.vp[:, :, :], add).then_inc(sem.cz, 1)
    V.wait_ge(sem.cu, 1)
    V.wait_ge(sem.c6, 1)
    V.tensor_tensor(T.nn[:, :, :], T.uu[:, :, :], T.xx[:, :, :], mult).then_inc(sem.cn, 1)
    V.wait_ge(sem.c7, 1)
    V.wait_ge(sem.cz, 1)
    V.tensor_tensor(T.dd[:, :, :], T.sq[:, :, :], T.zz[:, :, :], add).then_inc(sem.c8, 1)
    V.wait_ge(sem.c8, 1)
    V.reciprocal(T.rc[:, :, :], T.dd[:, :, :]).then_inc(sem.c9, 1)
    V.wait_ge(sem.c9, 1)
    V.wait_ge(sem.cn, 1)
    V.tensor_tensor(T.pp[:, :, :], T.nn[:, :, :], T.rc[:, :, :], mult).then_inc(sem.c10, 1)
    V.wait_ge(sem.c10, 1)
    V.tensor_tensor(T.yb[:, b0:b0 + 2, :], T.mv[:, :, 2 * F:3 * F], T.pp[:, :, :], sub).then_inc(sem.cw, 1)

    if lead:
        S.wait_ge(sem.cu, 1)
        S.activation(T.mvo[:, :, 0, :], T.uu[:, :, :], Act.Copy, scale=0.25).then_inc(sem.cv, 1)
        S.wait_ge(sem.cz, 1)
        S.activation(T.mvo[:, :, 1, :], T.zz[:, :, :], Act.Identity, bias=E * E / 4, scale=L / 2).then_inc(sem.cv, 1)
        g.wait_ge(sem.cv, 2)
        g.remote_dma(T.mvl[:, :, :], T.mvo[:, 1 - idx, :, :], sem.amo, sem.sent, pid, rid, _mask(on_eng))

    g.wait_ge(sem.cw, 1)
    g.remote_dma_fused(
        [RemoteDMATransfer(dst_ids=[dst(mine[i])], dma_engine_mask=_mask(eng[i] if i in eng else on_eng), remote_sem=sem.a3,
                           src=T.yb[:, b0:b0 + 2, :], dst=T.yb[:, b0:b0 + 2, :]) for i in range(len(mine)) if i != j],
        local_sem=sem.s3)

    if lead:
        Q.wait_ge(sem.cv, 2)
        Q.wait_ge(sem.s3, n_off + n_on)
        Q.dma_start(T.mo[:, :], T.mvo[:, idx, 0, :]).then_inc(sem.smv, 16)
        Q.dma_start(T.vo[:, :], T.mvo[:, idx, 1, :]).then_inc(sem.smv, 16)
    else:
        Q.wait_ge(sem.amo, n_on)
        Q.wait_ge(sem.s3, n_off + n_on)
        Q.dma_start(T.mo[:, :], T.mvl[:, 0, :]).then_inc(sem.smv, 16)
        Q.dma_start(T.vo[:, :], T.mvl[:, 1, :]).then_inc(sem.smv, 16)

    Q.wait_ge(sem.cw, 1)
    Q.wait_ge(sem.a3, n_off + n_on)
    Q.dma_start(T.y[:, :], T.yb[:, :, :]).then_inc(sem.sy, 16)
    Q.wait_ge(sem.smv, 32)
    Q.wait_ge(sem.sy, 16)
    g.wait_ge(sem.sent, 3 * n_off + 3 * n_on)
    g.wait_ge(sem.s3, n_off + n_on)
